import numpy as np, ml_dtypes
CORES = [2,3,42,43,82,83,122,123]
N = 8
BF = ml_dtypes.bfloat16
C, WS, WE, CAP, RO = 256, 2048, 4096, 32, 3
M, H = 16 * C, 8 * C
PL = np.arange(16)[:, None]
def tables(rng):
    amp = rng.choice(np.array([30, 100, 255]), (N, 8, 1, 1))
    e = np.floor((2 * rng.random((N, 8, 16, WS)) - 1) * amp).astype(np.int64)
    return np.clip(rng.integers(0, 256, (N, 8, 1, WS)) + e, 0, 255), rng.integers(0, 64, (N, 8, 16, WE)), rng.integers(0, 16, (N, 8, 16, 2))
def still(rng):
    return rng.integers(0, 41, (N, 8, 16, WS)), rng.integers(41, 64, (N, 8, 16, WE)), rng.integers(0, 16, (N, 8, 16, 2))
def chains(rng, K, keys, td):
    L = np.full((N, 8, 16, C), -1, np.int64); n = np.zeros((N, 8, C), np.int64)
    for g in range(8):
        low = [rng.permutation(H)[:int(K[g, r])] for r in range(N)]
        for r in range(N):
            lo = low[r]; hi = rng.permutation(low[(r - 1) % N]) + H
            o = np.argsort(keys[r, g].reshape(-1))[:len(lo) + len(hi) - 4 * C]
            m = 4 + np.bincount(o // 12, minlength=C)
            c0 = np.flatnonzero(td[r, g] == 0); c1 = np.flatnonzero(td[r, g] == 1)
            A = np.full((16, C), -1, np.int64)
            A[m[c0] - 1, c0] = lo[:len(c0)]; A[m[c1] - 1, c1] = hi[:len(c1)]
            A[(PL < m) & (A < 0)] = rng.permutation(np.concatenate([lo[len(c0):], hi[len(c1):]]))
            L[r, g] = A; n[r, g] = m
    return L, n
def monos(rng, n, low):
    z = rng.integers(0, 64, (N, 8, 16, C)); t = np.where(low, rng.integers(0, 8, low.shape), rng.integers(8, 64, low.shape))
    return np.where(PL == n[:, :, None, :] - 1, t[:, :, None, :], z)
def pack(tb, L, n, z):
    z = np.where(PL < n[:, :, None, :], z, 0); b = [np.ascontiguousarray(v.reshape(N, 128, -1)).astype(np.float32).astype(BF) for v in tb]
    return {"spr": b[0], "bar": b[1], "wt": b[2], "lam": np.ascontiguousarray(L.reshape(N, 128, C)).astype(np.int32), "mon": np.ascontiguousarray(z.reshape(N, 128, C)).astype(np.int32), "cnt": n.astype(np.int32)}
def anyway():
    return np.full((N, 8, C), -1)
def bring(A, v, k, c):
    i, j = np.nonzero(A == v); i, j = int(i[0]), int(j[0])
    A[i, j] = A[k, c]; A[k, c] = v
def crowd(rng, spr, wt, L, n, z):
    spr[:, 4, 0] = rng.integers(0, 256, (N, WS)); spr[:, 4, 1] = 32
    wt[:, 4] = 0; wt[:, 4, 0, 0] = 1; wt[:, 4, 1, 1] = 1
    for r in range(0, N, 2):
        A, A1 = L[r, 4], L[r + 1, 4]; v = int(np.min(A[A >= 0])); A1[A1 == v + H] = H; A[A == v] = 0
    tails = {}
    for s in range(1, N, 2):
        A = L[s, 4]; x = rng.permutation(A[A >= 0]); x = rng.permutation(x[np.unique(x >> 3, return_index=True)[1]])
        lo = x[x < H][:CAP]; hi = np.concatenate([np.array([H]), x[(x >= H) & ((x >> 3) != C)]])[:CAP]; tails[s] = (lo, hi)
        for v, c in zip(np.concatenate([lo, hi]), rng.permutation(C)):
            k = int(n[s, 4, c]) - 1; bring(L[s, 4], v, k, c); z[s, 4, k, c] = 0
    for r in range(0, N, 2):
        s0, s1 = (r - 1) % N, r + 1; lo, hi = tails[s0][0], tails[s1][1]
        o = 1 + rng.permutation(C - 2); a = np.concatenate([np.array([C - 1]), o[:2 * CAP - 1]]); q = np.insert(o[2 * CAP - 1:4 * CAP - 2], CAP, 0)
        for m, v in enumerate(np.concatenate([lo + H, hi - H])):
            bring(L[r, 4], v, 15 if m == 0 else int(rng.integers(0, n[r, 4, a[m]])), a[m])
        spr[s0, 4, 0, lo >> 3] = q[:CAP]; spr[s1, 4, 0, hi >> 3] = q[CAP:]; spr[s1, 4, :, C] = 0
def setup_inputs(rng):
    L, n = chains(rng, rng.integers(3 * C, 6 * C + 1, (8, N)), rng.random((N, 8, C, 12)) + 0.4 * rng.random((N, 8, C, 1)), anyway())
    low = rng.random((N, 8, C)) < rng.choice(np.array([0.1, 0.3, 0.5, 0.8]), (N, 8, 1))
    return pack(tables(rng), L, n, monos(rng, n, low))
def setup_inputs_room(rng):
    ch = np.array([0, 1, CAP - 1, CAP, CAP + 1, C // 2]); td = anyway(); low = np.zeros((N, 8, C), bool)
    for r in range(N):
        for g in range(8):
            a, b = int(rng.choice(ch)), int(rng.choice(ch))
            if r == 0: a, b = (CAP, CAP + 1, CAP - 1, 1, 0, C // 2, CAP, CAP + 1)[g], (CAP + 1, CAP, C // 2, 0, 1, CAP - 1, CAP + 1, CAP)[g]
            o = rng.permutation(C); td[r, g, o[:a]] = 0; td[r, g, o[a:a + b]] = 1; low[r, g, o[:a + b]] = True
    L, n = chains(rng, rng.integers(3 * C, 6 * C + 1, (8, N)), rng.random((N, 8, C, 12)), td)
    return pack(still(rng), L, n, monos(rng, n, low))
def setup_inputs_ties(rng):
    spr, bar, wt = tables(rng)
    for r in range(N):
        for g in range(8):
            P = int(rng.choice(np.array([4, 16, 64])))
            if r == 0: P = (4, 16, 64, 4, 16, 64, 16, 4)[g]
            top = np.argsort(np.argsort(rng.random((16, P)), axis=0), axis=0) < rng.integers(7, 11, (1, P))
            pat = rng.integers(0, 101, (16, 1)) + np.where(top, rng.choice(np.array([20, 21, 40]), (1, P)), 0)
            pat[:, 0] = pat[:, 0] - np.where(top[:, 0], pat[:, 0] - np.min(pat, axis=1), 0)
            spr[r, g] = pat[:, np.where(rng.random(WS) < 0.4, 0, rng.integers(0, P, WS))]
    bar = np.broadcast_to(rng.choice(np.array([0, 19, 20, 21, 40]), (N, 8, 1, WE)), bar.shape)
    L, n = chains(rng, rng.integers(3 * C, 6 * C + 1, (8, N)), rng.random((N, 8, C, 12)), anyway())
    return pack((spr, bar, wt), L, n, rng.choice(np.array([0, 1, 7, 8, 9, 15, 16, 56, 60, 63]), (N, 8, 16, C)))
def setup_inputs_clash(rng):
    spr, bar, wt = still(rng); wt[:, :3, :, 0] = 0; wt[:, 3] = 0; wt[:, 3, 0] = 1; wt[:, 3, 1] = rng.integers(0, 3, (N, 2))
    spr[::2, 5] = rng.integers(0, 2, (N // 2, 16, WS)); spr[1::2, 5] = rng.integers(245, 256, (N // 2, 16, WS))
    wt[1::2, 5, :, 0] = np.where(np.arange(16) < 12, 15, 10); wt[1::2, 5, 0, 1] = 15
    keys = rng.random((N, 8, C, 12)) + 2 * rng.integers(0, 2, (N, 8, C, 1))
    keys[:, 0:3:2, 0, :6] = -1; keys[:, 0:3:2, 0, 6:] = 9; keys[:, 1, 0] = -1
    keys[:, 4:6] = rng.random((N, 2, C, 12)); keys[:, 4:6, :, 0] = -1; keys[:, 4:6, :, 11] = 9
    keys[::2, 4, C - 1] = -1
    L, n = chains(rng, rng.integers(3 * C, 6 * C + 1, (8, N)), keys, anyway())
    for r in range(N):
        kk, cc = np.nonzero(L[r, 0] >= H); i = int(rng.integers(0, len(kk))); v = int(L[r, 0, kk[i], cc[i]])
        L[r, 0, kk[i], cc[i]] = L[r, 0, 0, 0]; L[r, 0, 0, 0] = v
    for r in range(N):
        v = int(L[(r + 1) % N, 0, 0, 0]) - H; kk, cc = np.nonzero(L[r, 0] == v); t = int(n[r, 0, 1]) - 1
        L[r, 0, kk[0], cc[0]] = L[r, 0, t, 1]; L[r, 0, t, 1] = v
    low = rng.random((N, 8, C)) < 0.3; low[:, :3, 0] = False; low[:, :3, 1] = True
    low[:, 4] = False; low[::2, 5] = False; low[1::2, 5] = rng.random((N // 2, C)) < 0.5
    z = monos(rng, n, low); crowd(rng, spr, wt, L, n, z)
    return pack((spr, bar, wt), L, n, z)
def setup_inputs_full(rng):
    K = rng.integers(2 * C, 8 * C + 1, (8, N)); o = rng.permutation(8)
    K[o[0]] = 8 * C; K[o[1]] = 2 * C; K[o[2]] = np.where(np.arange(N) % 2 == 0, 2 * C, 8 * C)
    L, n = chains(rng, K, rng.random((N, 8, C, 12)), anyway())
    low = rng.random((N, 8, C)) < rng.choice(np.array([0.0, 0.05, 0.2, 1.0]), (N, 8, 1))
    return pack(tables(rng), L, n, monos(rng, n, low))
def setup_inputs_spread(rng):
    spr = np.minimum(np.exp2(8 * rng.random((N, 8, 1, WS))) * (0.25 + rng.random((N, 8, 16, WS))), 255).astype(np.int64)
    bar = (np.exp2(6 * rng.random((N, 8, 16, WE))) - 1).astype(np.int64); wt = (np.exp2(4 * rng.random((N, 8, 16, 2))) - 1).astype(np.int64)
    L, n = chains(rng, rng.integers(2 * C, 8 * C + 1, (8, N)), rng.random((N, 8, C, 12)) + 1.5 * rng.random((N, 8, C, 1)), anyway())
    z = np.where(rng.random((N, 8, 1, C)) < 0.5, (64 * rng.random((N, 8, 16, C)) ** 4).astype(np.int64), 63 - (64 * rng.random((N, 8, 16, C)) ** 4).astype(np.int64))
    return pack((spr, bar, wt), L, n, z)
def check_inputs(d):
    bad = []
    for k, lo, hi in (("spr", 0, 255), ("bar", 0, 63), ("wt", 0, 15), ("lam", -1, M - 1), ("mon", 0, 63), ("cnt", 4, 16)):
        v = np.asarray(d[k]).astype(np.float64)
        if not np.all((v >= lo) & (v <= hi) & (v == np.floor(v))): bad.append("range of " + k)
    L = np.asarray(d["lam"]).astype(np.int64).reshape(N, 8, 16, C); z = np.asarray(d["mon"]).reshape(N, 8, 16, C); ok = PL < np.asarray(d["cnt"])[:, :, None, :]
    if np.any((L >= 0) != ok) or np.any((L != -1) & ~ok): bad.append("places of lam")
    if np.any((z != 0) & ~ok): bad.append("empty places of mon")
    have = np.zeros((N, 8, M), np.int64); r, g, k, c = np.nonzero(ok); np.add.at(have, (r, g, np.clip(L[r, g, k, c], 0, M - 1)), 1)
    if np.any(have > 1): bad.append("a name stands twice")
    if np.any(have[:, :, :H] != np.roll(have[:, :, H:], -1, axis=0)): bad.append("twins")
    return bad
def reference(spr, bar, wt, lam, mon, cnt):
    S, B, w = [v.astype(np.float32).astype(np.int64).reshape(N, 8, 16, -1) for v in (spr, bar, wt)]
    L = lam.astype(np.int64).reshape(N, 8, 16, C); z = mon.astype(np.int64).reshape(N, 8, 16, C); n = cnt.astype(np.int64)
    for t in range(RO):
        ok = PL < n[:, :, None, :]; x = np.where(ok, L, 0)
        i = ((((x + 77 * t) & (M - 1)) * (2 * z + 1)) >> 3) & (WS - 1)
        j = (((x[:, :, 1:] * (z[:, :, :-1] + 64)) >> 5) + 811 * z[:, :, 1:]) & (WE - 1)
        F = np.take_along_axis(S, i.reshape(N, 8, 1, 16 * C), 3).reshape(N, 8, 16, 16, C)
        E = np.take_along_axis(B, j.reshape(N, 8, 1, 15 * C), 3).reshape(N, 8, 16, 15, C)
        D = F[:, :, :, 1:] - F[:, :, :, :-1]
        up = np.add.reduce((D > E).astype(np.int64), axis=2) >= 9; down = np.add.reduce((-D > E).astype(np.int64), axis=2) >= 9
        s = np.zeros((N, 8, 17, C), np.int64); s[:, :, 1:16] = np.where(ok[:, :, 1:], 8 * up.astype(np.int64) - 8 * down.astype(np.int64), 0)
        z = np.where(ok, np.clip(z + s[:, :, :16] - s[:, :, 1:], 0, 63), 0)
        last = n - 1; zl = np.take_along_axis(z, last[:, :, None, :], 2)[:, :, 0]; ll = np.take_along_axis(L, last[:, :, None, :], 2)[:, :, 0]
        f = np.take_along_axis(F, last[:, :, None, None, :], 3)[:, :, :, 0]
        u1 = np.add.reduce(w[..., 0:1] * f, axis=2); u2 = np.add.reduce(w[..., 1:2] * f, axis=2)
        qn = (((u1 & 4095) * (u2 & 4095)) >> 5) & (C - 1)
        ev = [(zl < 8) & (ll < H), (zl < 8) & (ll >= H)]
        ev = [e & (np.add.accumulate(e.astype(np.int64), axis=2) <= CAP) for e in ev]
        sends = ev[0] | ev[1]
        moved = np.zeros((N, 8, C), bool); src = np.broadcast_to(PL, L.shape).copy(); grow = np.zeros((N, 8, C), np.int64); put = []
        for r in range(N):
            for g in range(8):
                p0, p1 = (r - 1) % N, (r + 1) % N
                a0 = np.flatnonzero(ev[0][p0, g]); a1 = np.flatnonzero(ev[1][p1, g])
                home = np.concatenate([np.full(len(a0), p0), np.full(len(a1), p1)]); hc = np.concatenate([a0, a1])
                name = np.concatenate([ll[p0, g, a0] + H, ll[p1, g, a1] - H]); q = qn[home, g, hc]; fm = f[home, g, :, hc].T
                kk, cc = np.nonzero(ok[r, g]); inv = np.zeros(M, np.int64); inv[L[r, g, kk, cc]] = 16 * cc + kk
                a = inv[name] >> 4; p = inv[name] & 15; m = np.arange(len(a))
                first = np.full(C, len(a)); np.minimum.at(first, a, m); np.minimum.at(first, q, m)
                good = (n[r, g, a] > 4) & (a != q) & (n[r, g, q] < 16) & ~sends[r, g, a] & ~sends[r, g, q] & (first[a] == m) & (first[q] == m)
                a, p, q, name, fm, home, hc = a[good], p[good], q[good], name[good], fm[:, good], home[good], hc[good]
                dist = np.add.reduce(np.abs(F[r, g][:, :, q] - fm[:, None, :]), axis=0)
                b = np.argmin(np.where(PL < n[r, g, q], dist, 2 ** 20), axis=0)
                moved[home, g, hc] = True
                src[r, g][:, a] = PL + (PL >= p); src[r, g][:, q] = PL - (PL > b)
                grow[r, g, a] = -1; grow[r, g, q] = 1; put.append((r, g, b, q, name))
        src = np.minimum(np.where(moved[:, :, None, :], np.where(PL == 0, last[:, :, None, :], PL - 1), src), 15)
        L = np.take_along_axis(L, src, 2); z = np.take_along_axis(z, src, 2)
        z[:, :, 0] = np.where(moved, 16, z[:, :, 0])
        for r, g, b, q, name in put:
            L[r, g, b, q] = name; z[r, g, b, q] = 16
        n = n + grow; ok = PL < n[:, :, None, :]; L = np.where(ok, L, -1); z = np.where(ok, z, 0)
    return {"yl": L.reshape(N, 128, C).astype(np.float32), "yz": z.reshape(N, 128, C).astype(np.float32), "yn": n.astype(np.float32)}

import numpy as np
from concourse.bass import DstId, RemoteDMATransfer
from concourse.mybir import AluOpType as AL, AxisListType, ActivationFunctionType as AF

RO = 3
NEG = -float(2 ** 20)
SGN = -2 ** 31
BIG = 1610612736.0
MW = 98
SW = 336
WD = 4176
D0 = 8
PICK = "010000022020000001010001011000111110111111001000000011110011100001000010111010101101111110001010000100010000100100100000110110011100001000001010110001000000101110000001111001100000001011110010100"
BUMP = {}
CFG = {"d0": "A", "NP": 4, "SC": 8, "look": 0.03, "U": ["VV", "VV", "VV"]}
COST = {"fix": 0.06, "cyc": 0.00104, "g": 1.56, "sc": 3.8, "pe": 0.00052, "tt2": 2.0, "same": 0.06, "cross": 0.12, "net": 2.5}

f32, bf, i32, u16 = "float32", "bfloat16", "int32", "uint16"
SB = {
    "lami": ([128, 256], i32), "moni": ([128, 256], i32), "wts": ([128, 2], bf),
    "SP": ([128, 2064], bf), "BR": ([128, 4112], bf), "F": ([128, 4112], bf), "Bg": ([128, 4112], bf),
    "Ub": ([128, 256, 16], bf), "Db": ([128, 256, 16], bf), "W": ([128, WD + 4096], f32), "CV": ([128, 4096], f32),
    "S": ([128, SW], f32), "Y": ([128, SW], f32), "RT": ([128, SW], f32), "FW": ([128, SW], f32),
    "t0": ([128, 256], i32), "t1": ([128, 256], i32), "zz": ([128, 256], i32), "t2": ([128, 256], i32),
    "t3": ([128, 256], f32), "t4": ([128, 256], i32), "t5": ([128, 256], i32), "t6": ([128, 256], f32),
    "t7": ([128, 256], i32), "t8": ([128, 256], f32),
    "iu": ([128, 256], u16), "ju": ([128, 256], u16), "wu": ([128, 256], u16), "z2b": ([128, 256], bf),
    "sg": ([128, 272], bf), "s1": ([128, 256], bf), "s2": ([128, 256], bf), "sh": ([128, 256], bf),
    "sig": ([128, 256], bf), "d1": ([128, 256], f32), "tpl": ([128, 32], u16), "FT": ([128, 512], bf),
    "Bs": ([128, 256], bf), "se": ([128, 256], bf), "d0": ([128, 512], bf), "G": ([128, 1024], f32),
    "r4": ([128, 4], f32), "tpo": ([128, 4], u16), "csi": ([128, 4], f32), "csf": ([128, 4], f32), "csl": ([128, 8], u16),
    "fm": ([128, 64], bf), "RTg": ([128, 64], f32), "emp": ([128, 64], bf), "ui": ([128, 128], i32), "um": ([128, 128], i32),
    "nd": ([128, 128], f32), "fu": ([128, 512], bf),
    "row": ([128, 2, 64], bf), "fb": ([128, 64], bf), "nm": ([128, 128], f32), "rd": ([128, 128], bf), "so": ([128, 128], bf),
    "lst": ([128, 8], u16), "base": ([128, 16], f32), "E": ([128, 8, 2, 64], bf), "Dg": ([128, 8, 2, 16], bf),
    "fl": ([128, 128], bf), "sc": ([128, 64], f32), "mn": ([128, 16], f32), "off": ([128, 16], u16), "qv": ([128, 64], f32),
    "eb": ([128, 64], bf), "Saq": ([128, 192], f32), "X": ([128, 320], f32), "Mc": ([128, 64], f32), "NW": ([128, 192], f32),
    "Fq": ([128, 1024], bf), "Ab": ([128, 4, 16, 16], bf), "ks": ([128, 64], f32), "bi": ([128, 8], i32), "bu": ([128, 4], u16),
    "oc": ([128, 8], f32), "ocu": ([128, 4], u16),
    "yls": ([128, 256], f32), "yzs": ([128, 256], f32), "yns": ([8, 256], f32),
    "pi": ([128, 4], i32), "col": ([128, 16], f32), "rr": ([128, 256], f32), "zer": ([128, 8, 16], bf),
    "MB": ([128, 24, 8, 16], bf), "MF": ([128, 6, 8, 16], f32), "Z": ([128, 144], bf), "ones": ([128, 256], bf),
    "dl": ([128, 128], bf), "rst": ([128, 128], bf), "rs2": ([128, 128], f32), "TRI": ([128, 8, 2, 16], bf),
    "cb": ([128, 5, 64], bf), "cneg": ([128, 64], f32), "T3": ([128, 48], f32), "dum": ([128, 16], f32),
    "c32": ([128, 64], f32), "cl": ([128, 2], u16), "dj": ([128, 256], f32),
}
for _t in range(RO):
    SB["snd%d" % _t] = ([128, 2, MW], u16)
    SB["L%d" % _t] = ([128, 2, MW], u16)
    SB["sm%d" % _t] = ([128, 16], f32)
    SB["ak%d" % _t] = ([128, 4], f32)
PS = {"H0": [128, 32, 16], "H1": [128, 32, 16], "H2": [128, 32, 16], "CN": [128, 512],
      "M0": [128, 512], "M1": [128, 512], "M2": [128, 512], "M3": [128, 512]}
SCRATCH = {k: ("sbuf", v[0], v[1]) for k, v in SB.items()}
SCRATCH.update({k: ("psum", v, f32) for k, v in PS.items()})
DMAS = ["lam", "mon", "spr", "bar", "wt", "yl", "yz", "yn"]
SEMAPHORES = (["qV", "qA", "qP", "qG", "sent"] + ["d_" + k for k in DMAS]
              + ["%s%d%d" % (k, s, t) for k in ("m", "a") for s in range(2) for t in range(RO)])
SHAPE = {k: v[0] for k, v in SB.items()}
SHAPE.update(PS)
DT = {k: v[1] for k, v in SB.items()}
DT.update({k: f32 for k in PS})
GRID = {k: np.arange(int(np.prod(v[1:]))).reshape(v[1:]) for k, v in SHAPE.items()}


def a(name, *idx):
    return {"n": name, "i": (slice(None),) + idx}


def s(lo, hi, st=None):
    return slice(lo, hi, st)


AllS = slice(None)


def ind(win, off):
    return {"n": win["n"], "i": win["i"], "off": off}


def span(x):
    cols = GRID[x["n"]][x["i"][1:]]
    return int(np.min(cols)), int(np.max(cols)) + 1, int(np.size(cols))


def count(x):
    return 16 * span(x["off"])[2] if "off" in x else span(x)[2]


def cost(v, C):
    e, k, n = v["e"], v["k"], v["n_"]
    if k == "dma":
        return v["args"][2]
    if k == "send":
        return 0.3
    if k == "recv":
        return C["net"]
    if e == "P":
        return 0.01 + max(64, n) * v["m_"] * C["pe"]
    if e == "G":
        return 0.17 + 2 * n * C["cyc"]
    m = {"g": C["g"], "sc": C["sc"], "t2": C["tt2"]}.get(v["m_"], v["m_"])
    return C["fix"] + (0.02 if e == "A" else 0.0) + max(64, n * m) * C["cyc"]


def program():
    ops = []

    def form(eng, kind, out, ins, args):
        n, m = 0, 1
        if kind not in ("dma", "send", "recv"):
            n = count(ins[0]) if kind == "red" else count(ins[1]) if kind == "mm" else count(out)
            narrow = all(DT[x["n"]] in (bf, u16) for x in [out] + ins[:2 if kind in ("tt", "scan") else 1])
            if kind == "mm":
                m = 4 if DT[ins[1]["n"]] == f32 else 1
            elif "off" in out:
                m = "sc"
            elif any("off" in x for x in ins):
                m = "g"
            elif kind == "tt":
                m = 1 if ins[0]["n"] in PS or ins[1]["n"] in PS else "t2" if narrow else 2
            elif kind in ("cp", "ts", "scan", "ms") and narrow:
                m = 0.5
        return {"e": eng, "k": kind, "o": out, "in": ins, "args": args, "n_": n, "m_": m}

    def put(*forms, **kw):
        ops.append({"alt": list(forms), "after": kw.get("after")})

    def CP(out, x):
        return form("V", "cp", out, [x], ())

    def TS(out, x, s1, op0, s2=None, op1=None):
        return form("V", "ts", out, [x] + [v for v in (s1, s2) if isinstance(v, dict)], (s1, op0, s2, op1))

    def ACT(out, x, fn, bias=None, scale=None):
        return form("A", "act", out, [x] + [v for v in (bias, scale) if isinstance(v, dict)], (fn, bias, scale))

    def IOTA(out, pat, base, ch):
        return form("G", "iota", out, [], (pat, base, ch))

    def SEL(out, x, pat, op, fill, base, ch):
        return form("G", "sel", out, [x], (pat, op, fill, base, ch))

    def cp(out, x):
        put(CP(out, x))

    def ts(*v):
        put(TS(*v))

    def act(out, x, fn, bias=None, scale=None):
        put(ACT(out, x, fn, bias, scale))

    def tt(out, x, y, op):
        put(form("V", "tt", out, [x, y], (op,)))

    def scan(out, x, y, init, op0, op1):
        put(form("V", "scan", out, [x, y] + ([init] if isinstance(init, dict) else []), (init, op0, op1)))

    def ms(out, v):
        fs = [form("V", "ms", out, [], (v,))]
        if v == int(v) and abs(v) < 2 ** 24:
            fs.append(IOTA(out, [[0, count(out)]], int(v), 0))
        put(*fs)

    def lin(out, x, scale=1.0, bias=0.0, first="A"):
        if scale == 1.0 and bias == 0.0:
            fs = [ACT(out, x, AF.Copy), CP(out, x)]
        else:
            fs = [ACT(out, x, AF.Identity, bias, scale), TS(out, x, scale, AL.mult, bias, AL.add)]
        put(*(fs if first == "A" else fs[::-1]))

    def sgn(out, x):
        put(ACT(out, x, AF.Sign), TS(out, x, -1.0, AL.max, 1.0, AL.min))

    def spread(out, x):
        put(ACT(out, x, AF.Silu), CP(out, x))

    def mm(out, l, r, start, stop):
        put(form("P", "mm", out, [l, r], (start, stop)))

    def mms(out, pairs, start=True, stop=True):
        for n, (l, r) in enumerate(pairs):
            mm(out, l, r, start and n == 0, stop and n == len(pairs) - 1)

    names = ["I", "nI", "I2", "nI2", "Dw", "Ia", "Ib", "I65", "nI16", "M8", "Bo", "nBo", "nB32", "pB32",
             "LT", "GT", "Rs", "R0", "R1", "W1", "W2", "Ih", "nIh"]
    M = {k: a("MB", n) for n, k in enumerate(names)}
    fn = ["I", "D", "U", "Bo", "Z0", "I17"]
    MFn = {k: a("MF", n) for n, k in enumerate(fn)}
    cn = ["k", "k8", "km8", "z1", "z2", "y1", "y2", "tpa", "tpb", "ia", "ib", "is0", "is15"]
    col = {k: a("col", s(n, n + 1)) for n, k in enumerate(cn)}

    def sel(r):
        return a("Z", s(15 - r, 143 - r))

    CH = s(1, 257)
    put(form("S", "dma", a("lami"), [], ("lam", 0, 2.2)))
    put(form("A", "dma", a("moni"), [], ("mon", 0, 2.2)))
    put(form("S", "dma", a("SP", s(16, 2064)), [], ("spr", 0, 4.0)))
    put(form("A", "dma", a("BR", s(16, 4112)), [], ("bar", 0, 7.0)))
    put(form("S", "dma", a("wts"), [], ("wt", 0, 7.0)))

    P2 = [[-16, 8], [-1, 16]]
    zer = a("zer")
    ms(zer, 0.0)
    ms(a("ones"), 1.0)
    put(IOTA(a("pi", s(0, 1)), [[0, 1]], 0, 1))
    ts(a("pi", s(1, 2)), a("pi", s(0, 1)), 15, AL.bitwise_and)
    cp(col["k"], a("pi", s(1, 2)))
    put(SEL(M["I"], zer, P2, AL.not_equal, 1.0, 0, 1))
    for d, k, v in ((M, "Ia", 24576.0), (M, "Ib", 1376.0), (M, "I2", 2.0), (M, "nI2", -2.0), (M, "nI", -1.0), (M, "I65", 65.0),
                    (M, "nI16", -1.0 / 16), (M, "Ih", 0.5), (M, "nIh", -0.5), (MFn, "I", 1.0), (MFn, "I17", 2.0 ** -17)):
        put(SEL(d[k], zer, P2, AL.not_equal, v, 0, 1), ACT(d[k], M["I"], AF.Identity, None, v), TS(d[k], M["I"], v, AL.mult))

    def part(buf, n, lo, hi):
        return a(buf, n, AllS, s(lo, hi))

    for buf, n, v in (("MB", names.index("Dw"), 1.0 / 128), ("MF", fn.index("D"), 1.0)):
        ms(part(buf, n, 0, 1), 0.0)
        put(SEL(part(buf, n, 1, 16), a("zer", AllS, s(1, 16)), [[-16, 8], [-1, 15]], AL.not_equal, v, 0, 1))
    ms(part("MF", fn.index("U"), 15, 16), 0.0)
    put(SEL(part("MF", fn.index("U"), 0, 15), a("zer", AllS, s(0, 15)), [[-16, 8], [-1, 15]], AL.not_equal, 1.0, -1, 1))
    n8 = names.index("M8")
    put(SEL(M["M8"], zer, P2, AL.not_equal, 8.0, 0, 1), ACT(M["M8"], M["I"], AF.Identity, None, 8.0), TS(M["M8"], M["I"], 8.0, AL.mult))
    put(SEL(part("MB", n8, 0, 15), part("MB", n8, 0, 15), [[-16, 8], [-1, 15]], AL.not_equal, -8.0, -1, 1))
    put(SEL(M["Bo"], a("ones", s(0, 128)), [[-16, 8], [0, 16]], AL.is_ge, 0.0, 0, 1))
    put(SEL(M["Bo"], M["Bo"], [[16, 8], [0, 16]], AL.is_ge, 0.0, 15, -1))
    for d, k, v in ((M, "nBo", -1.0), (M, "nB32", -32.0), (M, "pB32", 32.0), (MFn, "Bo", 1.0)):
        lin(d[k], M["Bo"], v)
    put(SEL(M["LT"], M["Bo"], P2, AL.is_gt, 0.0, 0, 1))
    put(SEL(M["GT"], M["Bo"], [[16, 8], [1, 16]], AL.is_gt, 0.0, 0, -1))
    put(SEL(M["R0"], zer, [[-16, 8], [0, 16]], AL.not_equal, 1.0, 0, 1))
    put(SEL(M["R1"], zer, [[-16, 8], [0, 16]], AL.not_equal, 1.0, -1, 1))
    nr_ = names.index("Rs")
    ms(part("MB", nr_, 2, 16), 0.0)
    put(SEL(part("MB", nr_, 0, 1), a("zer", AllS, s(0, 1)), [[-16, 8]], AL.not_equal, -0.5, -4, 1))
    put(SEL(part("MB", nr_, 1, 2), a("zer", AllS, s(0, 1)), [[-16, 8]], AL.not_equal, 0.5, -15, 1))
    ms(a("Z"), 0.0)
    lin(a("Z", s(15, 143, 16)), part("MB", names.index("Bo"), 0, 1), first="V")
    lin(MFn["Z0"], sel(0))
    for k, m_, b_ in (("k8", 1.0, 8.0), ("km8", 1.0, -8.0), ("tpa", 16.0, 15.0), ("tpb", 16.0, 14.0),
                      ("ia", 2.0, 2.0), ("ib", 2.0, 34.0)):
        lin(col[k], col["k"], m_, b_, first="V")
    ts(col["is15"], col["k"], 15.0, AL.is_equal)
    ts(col["is0"], col["k"], 0.0, AL.is_equal, 97.0, AL.mult)
    for k, m_, b_ in (("z1", 128.0, -241.0), ("z2", 128.0, -225.0), ("y2", 2.0 ** 20, -2.0 ** 21),
                      ("y1", 2.0 ** 20, -2.0 ** 21 - 262080.0)):
        lin(col[k], col["is15"], m_, b_, first="V")
    ms(a("SP", s(0, 16)), 1024.0)
    ms(a("BR", s(0, 16)), 4096.0)
    ms(a("sg", s(0, 1)), 0.125)
    ms(a("F", s(0, D0)), 0.0)
    ms(a("F", s(D0 + 4096, 4112)), 0.0)
    ms(a("Bg", s(0, D0)), 0.0)
    ms(a("Bg", s(D0 + 4096, 4112)), 512.0)
    put(IOTA(a("cb", 0, s(0, 16)), [[512, 16]], 0, 0))
    put(IOTA(a("rr"), [[0, 16], [1, 16]], 0, 0))
    ts(a("dl"), a("rr", s(0, 128)), col["k"], AL.is_equal)
    put(TS(a("rst"), a("rr", s(0, 128)), 0.0, AL.is_gt), ACT(a("rst"), a("rr", s(0, 128)), AF.Sign))
    lin(a("rs2", s(0, 64)), a("rst", s(0, 64)), 2.0 ** 24, -2.0 ** 23)
    lin(a("rs2", s(64, 128)), a("rst", s(0, 64)), -2.0 ** 24, 2.0 ** 23)
    ts(a("TRI"), a("rr"), col["k"], AL.is_gt)
    ts(a("TRI", s(0, 4), 1), a("rr", s(0, 64)), col["k"], AL.is_ge)
    lin(a("cb", 1), a("dl", s(0, 64)), 2.0 ** 22, -2.0 ** 22)
    ms(a("cb", 2, s(0, 32)), 262144.0)
    ms(a("cb", 2, s(32, 64)), -262144.0)
    put(IOTA(a("cb", 3), [[0, 4], [1, 16]], 0, 0))
    lin(a("cb", 4), a("ones", s(0, 64)), col["is0"])
    ts(a("cneg"), a("ones", s(0, 64)), col["is15"], AL.mult, NEG + 65, AL.mult)
    ts(a("T3", s(0, 16)), a("rr", s(0, 16)), col["k"], AL.is_gt)
    ts(a("T3", s(16, 32)), a("rr", s(0, 16)), col["k"], AL.is_le)
    lin(a("T3", s(32, 48)), a("dl", s(0, 16)))
    put(IOTA(a("dum", s(0, 8)), [[0, 2], [16, 4]], 257, 0))
    put(IOTA(a("dum", s(8, 12)), [[16, 4]], 4097, 0))
    lin(a("dum", s(0, 12)), a("dum", s(0, 12)), 1.0, col["k"])
    ts(a("pi", s(2, 3)), a("pi", s(0, 1)), 3, AL.bitwise_and)
    ts(a("cl", s(0, 1)), a("pi", s(2, 3)), 16.0, AL.mult, 15.0, AL.add)
    ms(a("c32"), 8192.0)
    ms(a("base", s(12, 16)), 0.0)
    for w, v in (("S", 0.0), ("Y", 0.0), ("RT", float(2 ** 20)), ("FW", 8192.0)):
        ms(a(w, s(0, 1)), v)
        ms(a(w, s(257, SW)), v)
    ms(a("W", s(4096, WD)), 31.0)
    ts(M["W1"], M["Bo"], a("wts", s(0, 1)), AL.mult)
    ts(M["W2"], M["Bo"], a("wts", s(1, 2)), AL.mult)

    put(IOTA(a("dj"), [[16, 256]], WD, 0))
    lin(a("dj"), a("dj"), 1.0, col["k"])
    ts(a("t7"), a("lami"), 16383, AL.bitwise_and)
    tt(a("t8"), a("t7"), a("dj"), AL.min)
    cp(a("wu"), a("t8"))
    n = 256 // CFG["SC"]
    for p in range(CFG["SC"]):
        put(IOTA(a("CV", s(16 * n * p, 16 * n * (p + 1))), [[1, n], [0, 16]], 32 + n * p, 0))
        spread(ind(a("W"), a("wu", s(n * p, n * (p + 1)))), a("CV", s(16 * n * p, 16 * n * (p + 1))))

    for t in range(RO):
        snd, L, sm, ak = "snd%d" % t, "L%d" % t, "sm%d" % t, "ak%d" % t
        S, Y = a("S", CH), a("Y", CH)
        if t == 0:
            ts(a("t1"), a("lami"), 4095 + SGN, AL.bitwise_and)
            ts(a("zz"), a("moni"), 2.0, AL.mult, 1.0, AL.add)
            ts(Y, a("lami"), 128.0, AL.mult)
        else:
            ts(a("t0"), S, 9856.0 * t - 64, AL.add)
            ts(a("t1"), a("t0"), 7, AL.arith_shift_right, 4095 + SGN, AL.bitwise_and)
            ts(a("zz"), a("t0"), 127, AL.bitwise_and)
            act(a("t8"), S, AF.Identity, bias=BIG)
            act(Y, a("t8"), AF.Identity, bias=-BIG - 128)
        tt(a("t2"), a("t1"), a("zz"), AL.mult)
        ts(a("t7"), a("t2"), 3, AL.arith_shift_right, 2047 + SGN, AL.bitwise_and)
        ts(a("iu"), a("t7"), 16.0, AL.add)
        ts(a("z2b"), a("zz"), -1.0, AL.add)
        mms(a("M0", s(0, 256)), [(M["I"], a("ones")), (M["Dw"], a("z2b"))])
        mms(a("M1", s(0, 256)), [(M["Ia"], a("z2b")), (M["Ib"], a("z2b"))])
        tt(a("t3"), a("M0", s(0, 256)), Y, AL.mult)
        tt(a("t4"), a("M1", s(0, 256)), a("t3"), AL.add)
        ts(a("t5"), a("t4"), 6, AL.arith_shift_right, 4095 + SGN, AL.bitwise_and)
        ts(a("ju"), a("t5"), 16.0, AL.add)
        n = 256 // CFG["NP"]
        for q in range(CFG["NP"]):
            lin(a("F", s(D0 + 16 * n * q, D0 + 16 * n * (q + 1))), ind(a("SP"), a("iu", s(n * q, n * q + n))))
        for q in range(CFG["NP"]):
            lin(a("Bg", s(D0 + 16 * n * q, D0 + 16 * n * (q + 1))), ind(a("BR"), a("ju", s(n * q, n * q + n))), 4.0, 2.0, "V")
        sg = a("sg", CH)
        act(sg, Y, AF.Sign, bias=0.5)
        mms(a("M3", s(256, 272)), [(M["I"], a("cb", 0, s(0, 16)))] + [(sel(r), a("sg", s(1 + r, 257, 16))) for r in range(16)])
        mms(a("M3", s(0, 256)), [(M["Bo"], sg), (M["nBo"], a("sg", s(0, 256)))])
        mms(a("M2", s(0, 256)), [(M["nI16"], a("z2b")), (M["M8"], sg)])
        mms(a("M2", s(256, 512)), [(MFn["I17"], Y), (M["M8"], sg)])
        ts(a("tpl", s(0, 16)), a("M3", s(256, 272)), 0.5, AL.mult, col["tpa"], AL.add)
        ts(a("tpl", s(16, 32)), a("M3", s(256, 272)), 0.5, AL.mult, col["tpb"], AL.add)
        dv = CFG["d0"] == "V"
        lin(a("d1"), a("M3", s(0, 256)), 1.0 / 16384, (-2.0 if dv else -1.0) + 1.0 / 512)
        act(a("s1"), a("M2", s(0, 256)), AF.Sign, bias=col["z1"], scale=16.0)
        act(a("s2"), a("M2", s(0, 256)), AF.Sign, bias=col["z2"], scale=16.0)
        act(a("sh"), a("M2", s(256, 512)), AF.Sign, bias=col["y1"], scale=2.0 ** 17)
        act(a("RT", CH), a("M2", s(256, 512)), AF.Relu, bias=col["y2"], scale=2.0 ** 17)
        mms(a("CN", s(0, 256)), [(M["Bo"], a("s1"))])
        mms(a("CN", s(256, 512)), [(M["Rs"], sg)])
        lin(a("sig"), a("CN", s(0, 256)), -1.0, -15.0)
        lin(a("FW", CH), a("CN", s(256, 512)), 8192.0, 4096.0)
        if t == 0:
            put(ACT(a("t6"), Y, AF.Relu, None, -8192.0), TS(a("t6"), Y, -8192.0, AL.mult, 0.0, AL.max))
            tt(Y, Y, a("t6"), AL.subtract)
        lin(a("FT", s(0, 256)), ind(a("F"), a("tpl", s(0, 16))))
        lin(a("FT", s(256, 512)), ind(a("F"), a("tpl", s(16, 32))))
        tt(a("Bs"), ind(a("Bg"), a("tpl", s(0, 16))), a("sig"), AL.mult)
        mms(a("M3", s(0, 256)), [(M["I2"], a("FT", s(256, 512))), (M["nI2"], a("FT", s(0, 256))), (M["nIh"], a("Bs"))])
        sgn(a("se"), a("M3", s(0, 256)))
        for d, b, hk, bias in ((0, "M0", "nB32", 49.0), (1, "M1", "pB32", -911.0)):
            mms(a(b, s(0, 256)), [(M["Bo"], a("s1")), (M["pB32"], a("s2")), (M[hk], a("sh")), (M["Bo"], a("se"))])
            if dv:
                ts(a("d0", s(256 * d, 256 * d + 256)), a(b, s(0, 256)), bias, AL.is_lt, 2.0, AL.mult)
            else:
                act(a("d0", s(256 * d, 256 * d + 256)), a(b, s(0, 256)), AF.Sign, bias=bias, scale=-1.0)
        for j in range(4):
            d = j // 2
            Gj = a("G", s(256 * j, 256 * j + 256))
            f0 = form("V", "scan", Gj, [a("d0", s(256 * d, 256 * d + 256)), a("d1"), col["ib" if j % 2 else "ia"]],
                      (col["ib" if j % 2 else "ia"], AL.add, AL.add))
            if j % 2:
                put(f0, ACT(Gj, a("G", s(256 * j - 256, 256 * j)), AF.Identity, 32.0))
            else:
                put(f0)
            put(form("V", "red", a("r4", s(j, j + 1)), [Gj], ()))
        ts(a("tpo"), a("r4"), 8192.0, AL.mult, D0 + 4096.0, AL.min)
        ts(a("csl", s(0, 4)), a("r4"), 512.0, AL.mult, 257.0, AL.min)
        lin(a("csi"), a("r4"), 512.0)
        tt(a("csf"), a("csi"), a("dum", s(0, 4)), AL.min)
        cp(a("csl", s(4, 8)), a("csf"))
        cs0, cs1 = a("csl", s(0, 4)), a("csl", s(4, 8))
        lin(a("fm"), ind(a("F"), a("tpo")))
        lin(a("RTg"), ind(a("RT"), cs0))
        put(TS(a("emp"), ind(a("Bg"), a("tpo")), 300.0, AL.is_ge), ACT(a("emp"), ind(a("Bg"), a("tpo")), AF.Relu, -1.0, 1.0 / 256))
        mms(a("M0", s(0, 64)), [(M["W1"], a("fm")), (M["nI"], a("emp"))])
        mms(a("M0", s(64, 128)), [(M["W2"], a("fm")), (M["I"], a("emp"))])
        mms(a("M1", s(0, 64)), [(M["I"], a("cb", 2)), (MFn["Bo"], a("RTg"))])
        cp(a(snd, AllS, s(32, 64)), a("fm"))
        cp(a("ui"), a("M0", s(0, 128)))
        ts(a("um"), a("ui"), 4095 + SGN, AL.bitwise_and)
        tt(a("ui", s(0, 64)), a("um", s(0, 64)), a("um", s(64, 128)), AL.mult)
        ts(a("ui", s(64, 128)), a("ui", s(0, 64)), 1, AL.arith_shift_right, 4080 + SGN, AL.bitwise_and)
        ts(a(snd, AllS, s(0, 32)), a("ui", s(64, 128)), col["k8"], AL.add)
        ts(a(snd, AllS, s(64, 96)), a("M1", s(0, 64)), 1.0 / 128, AL.mult, 4096.0, AL.min)
        tt(a("nd", s(0, 64)), a("M1", s(0, 64)), a("dl", s(0, 64)), AL.mult)
        scan(a("nd", s(64, 128)), a("rst", s(0, 64)), a("nd", s(0, 64)), 0.0, AL.mult, AL.add)
        ts(a(snd, AllS, s(96, 98)), a("nd", s(79, 128, 16)), 1.0 / 128, AL.mult, 4096.0, AL.min)
        put(form("G", "send", None, [a(snd)], ("m", t)))
        sent = len(ops) - 1
        spread(ind(a("FW"), cs1), a("c32"))
        bank = [0]
        for c in range(8):
            hn = "H%d" % (bank[0] % 3)
            bank[0] += 1
            Dc = [(M["I2"], a("F", s(D0 + 512 * c, D0 + 512 + 512 * c))),
                  (M["nI2"], a("F", s(D0 - 1 + 512 * c, D0 + 511 + 512 * c)))]
            Bc = a("Bg", s(D0 + 512 * c, D0 + 512 + 512 * c))
            mms(a(hn), Dc + [(M["Ih"], Bc)])
            sgn(a("Db", s(32 * c, 32 * c + 32), s(1, 16)), a(hn, AllS, s(1, 16)))
            if CFG["U"][t][c // 4] == "V":
                tt(a("Ub", s(32 * c, 32 * c + 32)), a(hn), Bc, AL.is_gt)
            else:
                hn = "H%d" % (bank[0] % 3)
                bank[0] += 1
                mms(a(hn), Dc + [(M["nIh"], Bc)])
                sgn(a("Ub", s(32 * c, 32 * c + 32), s(1, 16)), a(hn, AllS, s(1, 16)))
            if c % 4 == 3:
                h = c // 4
                for o, src in ((256, "Db"), (0, "Ub")):
                    mms(a("CN", s(o + 128 * h, o + 128 * h + 128)),
                        [(sel(k), a(src, s(128 * h, 128 * h + 128), k)) for k in range(1, 16)])
        act(a("fu", s(256, 512)), a("CN", s(256, 512)), AF.Sign, bias=1.0)
        cut = [(0, 256)] if CFG["U"][t][0] == CFG["U"][t][1] else [(0, 128), (128, 256)]
        for lo, hi in cut:
            act(a("fu", s(lo, hi)), a("CN", s(lo, hi)), AF.Sign, bias=-8.5 if CFG["U"][t][lo // 128] == "V" else -1.0)
        mms(a("H0", s(0, 16)), [(M["I65"], a("ones")), (M["I"], a("z2b")), (M["M8"], a("fu", s(256, 512))),
                                (M["M8"], a("fu", s(0, 256)))])
        ts(a("t3"), a("H0", s(0, 16)), 65.0, AL.max, 191.0, AL.min)
        tt(S, a("t3"), Y, AL.add)
        for d in range(2):
            put(form("R", "recv", a(L, d), [], ("m", d, t)), after=sent)
        for d in range(2):
            lin(a("row", 0, s(32 * d, 32 * d + 32)), ind(a("W", s(0, WD)), a(L, d, s(96, 98))), 1.0, -31.0)
        ts(a("row", 1), a(L, AllS, s(0, 32)), col["km8"], AL.subtract, 1.0 / 16, AL.mult)
        cp(a("fb"), a(L, AllS, s(32, 64)))
        ts(a("nm", s(0, 64)), a(L, AllS, s(64, 96)), 128.0, AL.mult)
        cp(a("base", s(8, 12)), a(L, AllS, s(96, 98)))
        tt(a("rd"), a("row"), a("dl"), AL.mult)
        scan(a("so"), a("rst"), a("rd"), 0.0, AL.mult, AL.add)
        cp(a("lst"), a("so", s(15, 128, 16)))
        lin(a("base", s(0, 8)), a("so", s(15, 128, 16)))
        lin(a("fl"), ind(a("FW"), a("lst")))
        for e in range(8):
            j = e % 4
            ts(a("E", e, AllS, s(0, 64 - 16 * j)), a("row", AllS, s(16 * j, 64)), a("so", s(16 * e + 15, 16 * e + 16)),
               AL.is_equal, 8192.0, AL.mult)
        for v in range(2):
            tt(a("Dg", s(4 * v, 4 * v + 4)), a("E", s(4 * v, 4 * v + 4), AllS, s(0, 16)), a("TRI", s(4 * v, 4 * v + 4)), AL.mult)
        mm(a("M0", s(0, 64)), M["I"], a("cb", 1), True, False)
        for e in range(8):
            j = e % 4
            if j < 3:
                for u in range(2):
                    mm(a("M0", s(16 * j + 16, 64)), M["Bo"], a("E", e, u, s(16, 64 - 16 * j)), False, False)
        mms(a("M0", s(0, 64)), [(M["R0"], a("fl", s(0, 64))), (M["R1"], a("fl", s(64, 128)))]
            + [(M["Bo"], a("Dg", s(4 * v, 4 * v + 4), u)) for v in range(2) for u in range(2)], start=False)
        scan(a("sc"), a("rs2", s(0, 64)), a("M0", s(0, 64)), 0.0, AL.min, AL.max)
        tt(a(sm), ind(a("sc"), a("cl", s(0, 1))), a("base"), AL.add)
        put(form("G", "send", None, [a(sm, s(12, 16))], ("a", t)))
        acked = len(ops) - 1
        tt(a("mn", s(0, 12)), a(sm, s(0, 12)), a("dum", s(0, 12)), AL.min)
        cp(a("off", s(0, 12)), a("mn", s(0, 12)))
        for d, b in ((0, "M2"), (1, "M3")):
            lin(a("Fq", s(512 * d, 512 * d + 512)), ind(a("F"), a(L, d, s(0, 32))))
            for k in range(16):
                mm(a(b, s(k, 512, 16)), M["nI"], a("fb", s(32 * d, 32 * d + 32)), k == 0, False)
            mm(a(b), M["I"], a("Fq", s(512 * d, 512 * d + 512)), False, True)
            act(a("Ab", s(2 * d, 2 * d + 2)), a(b), AF.Abs, scale=16.0)
        mms(a("M2", s(0, 64)), [(M["I"], a("cb", 3))] + [(sel(r), a("Ab", AllS, r)) for r in range(16)])
        scan(a("ks"), a("rs2", s(64, 128)), a("M2", s(0, 64)), 0.0, AL.max, AL.min)
        cp(a("bi", s(0, 4)), a("ks", s(15, 64, 16)))
        ts(a("bi", s(4, 8)), a("bi", s(0, 4)), 15, AL.bitwise_and)
        cp(a("bu"), a("bi", s(4, 8)))
        tt(a("eb"), ind(a("Y"), a("lst", s(0, 4))), a("nm", s(0, 64)), AL.is_equal)
        lin(a("nm", s(64, 128)), a("nm", s(0, 64)), 1.0, 97.0)
        mms(a("M1", s(0, 64)), [(M["LT"], a("eb"))])
        mms(a("M1", s(64, 128)), [(M["GT"], a("eb"))])
        lin(a("Saq", s(0, 128)), ind(a("S"), a("lst")))
        lin(a("Saq", s(128, 192)), ind(a("S"), cs0))
        ts(a("Mc"), a("Saq", s(128, 192)), float(2 ** 20), AL.mult, NEG + 65, AL.max)
        tt(a("X", s(0, 64)), a("M1", s(0, 64)), a("Saq", s(0, 64)), AL.mult)
        tt(a("X", s(64, 128)), a("M1", s(64, 128)), a("Saq", s(0, 64)), AL.mult)
        mms(a("H1", s(0, 4)), [(M["I"], a("cb", 4)), (MFn["Z0"], a("RTg")), (MFn["D"], a("Saq", s(128, 192)))])
        tt(a("NW", s(128, 192)), a("H1", s(0, 4)), a("Mc"), AL.min)
        mms(a("H2", s(0, 4)), [(MFn["I"], a("cneg")), (MFn["I"], a("X", s(0, 64))), (MFn["U"], a("X", s(64, 128)))])
        lin(a("NW", s(0, 64)), a("H2", s(0, 4)))
        tt(a("X", s(256, 320)), ind(a("T3", s(32, 48)), a("bu")), a("nm", s(64, 128)), AL.mult)
        tt(a("X", s(128, 192)), ind(a("T3", s(0, 16)), a("bu")), a("Saq", s(64, 128)), AL.mult)
        tt(a("X", s(192, 256)), ind(a("T3", s(16, 32)), a("bu")), a("Saq", s(64, 128)), AL.mult)
        mms(a("M3", s(0, 64)), [(MFn["I"], a("X", s(256, 320))), (MFn["I"], a("X", s(128, 192))), (MFn["D"], a("X", s(192, 256)))])
        lin(a("NW", s(64, 128)), a("M3", s(0, 64)))
        cp(ind(a("S"), a("off", s(0, 4))), a("NW", s(0, 64)))
        for d in range(2):
            put(form("R", "recv", a(ak, s(2 * d, 2 * d + 2)), [], ("a", d, t)), after=acked)
        tt(a("oc", s(0, 4)), a(ak), a("csf"), AL.add)
        tt(a("oc", s(4, 8)), a("oc", s(0, 4)), a("dum", s(0, 4)), AL.min)
        cp(a("ocu"), a("oc", s(4, 8)))
        cp(ind(a("S"), a("ocu")), a("NW", s(128, 192)))
        cp(ind(a("S"), a("off", s(4, 8))), a("NW", s(64, 128)))
        if t < RO - 1:
            lin(a("qv"), a("row", 1), 1.0, 31.0)
            spread(ind(a("W", s(0, WD)), a("off", s(8, 12))), a("qv"))

    S = a("S", CH)
    ts(a("t0"), S, -64.0, AL.add)
    ts(a("t1"), a("t0"), 7, AL.arith_shift_right)
    ts(a("yls"), a("t1"), -1.0, AL.max)
    put(form("S", "dma", None, [a("yls")], ("yl", 1, 2.2)))
    ts(a("t2"), a("t0"), 1, AL.arith_shift_right, 63, AL.bitwise_and)
    cp(a("yzs"), a("t2"))
    put(form("S", "dma", None, [a("yzs")], ("yz", 1, 2.2)))
    act(a("sg", CH), S, AF.Sign)
    o8 = {"n": "M0", "i": (s(0, 8), s(0, 256))}
    mm(o8, a("Z", s(15, 143, 16)), a("sg", CH), True, True)
    act(a("yns"), o8, AF.Identity, bias=8.0, scale=0.5)
    put(form("A", "dma", None, [a("yns")], ("yn", 1, 2.2)))
    for op in ops:
        for v in op["alt"]:
            acc = ([(v["o"], True)] if v["o"] is not None else []) + [(x, False) for x in v["in"]]
            acc += [(x["off"], False) for x, _w in acc if "off" in x]
            v["acc"] = [(x["n"], 0, 512, True) if x["n"] in PS else (x["n"],) + span(x)[:2] + (w,) for x, w in acc]
    return ops


def choose(prog, pick):
    ops, f, hist = [], 0, {}
    for n, op in enumerate(prog):
        c = 0
        if len(op["alt"]) > 1:
            c = int(pick[f]) if f < len(pick) else 0
            f += 1
        v = dict(op["alt"][c])
        deps = set()
        for nm, lo, hi, w in v["acc"]:
            h = hist.setdefault(nm, [])
            for (m, l2, h2, w2) in h:
                if m != n and l2 < hi and lo < h2 and (w or w2):
                    deps.add(m)
            if w:
                h[:] = [z for z in h if not (lo <= z[1] and z[2] <= hi) or z[0] == n]
            h.append((n, lo, hi, w))
        v["deps"] = sorted(deps)
        v["all"] = v["deps"] + ([op["after"]] if op["after"] is not None else [])
        ops.append(v)
    return ops


def lag(x, y, C):
    return 0.0 if x["e"] == "P" and y["e"] == "P" else C["same"] if x["e"] == y["e"] else C["cross"]


def hold(op, c):
    return 0.05 if op["k"] == "dma" else 0.0 if op["e"] == "R" else c


def schedule(ops, bump, C):
    N = len(ops)
    c = [cost(v, C) for v in ops]
    succ = [[] for _ in range(N)]
    for n, op in enumerate(ops):
        for m in op["all"]:
            succ[m].append(n)
    pr = [0.0] * N
    for n in range(N - 1, -1, -1):
        pr[n] = c[n] + max([pr[m] + lag(ops[n], ops[m], C) for m in succ[n]] + [0.0])
    pr = [p + bump.get(n, 0.0) for n, p in enumerate(pr)]
    left = [len(op["all"]) for op in ops]
    ready = {e: {} for e in "VAPGSR"}
    for n in range(N):
        if left[n] == 0:
            ready[ops[n]["e"]][n] = 0.0
    free = {e: 0.0 for e in "VAPGSR"}
    end = [0.0] * N
    order = []
    for _ in range(N):
        t0, e = min((max(free[e], min(r.values())), e) for e, r in ready.items() if r)
        r = ready[e]
        n = max((v for v in r if r[v] <= t0 + CFG["look"]), key=lambda v: (pr[v], -v))
        st = max(free[e], r.pop(n))
        ops[n]["t"] = st
        end[n] = st + c[n]
        free[e] = st + hold(ops[n], c[n])
        order.append(n)
        for m in succ[n]:
            left[m] -= 1
            if left[m] == 0:
                ready[ops[m]["e"]][m] = max(end[v] + lag(ops[v], ops[m], C) for v in ops[m]["all"])
    return order, max(end)


def plan():
    ops = choose(program(), PICK)
    order, end = schedule(ops, BUMP, COST)
    pos = {n: p for p, n in enumerate(order)}
    known = {e: {} for e in "VAPGSR"}
    seen = {}
    for n in order:
        op = ops[n]
        e = op["e"]
        kn = known[e]
        op["w"] = []
        if e != "R":
            for m in sorted(op["deps"], key=lambda v: -pos[v]):
                pm = ops[m]
                if e == "P" and pm["e"] == "P":
                    continue
                key = m if pm["k"] in ("dma", "recv") else pm["e"]
                if kn.get(key, -1) >= pos[m]:
                    continue
                op["w"].append(m)
                pm["inc"] = True
                kn[key] = pos[m]
                for k2, v2 in seen[m].items():
                    if kn.get(k2, -1) < v2:
                        kn[k2] = v2
        seen[n] = dict(kn) if e != "R" else {}
    cnt = {e: 0 for e in "VAPG"}
    for n in order:
        op = ops[n]
        if op.get("inc") and op["k"] not in ("dma", "recv"):
            cnt[op["e"]] += 1
            op["n"] = cnt[op["e"]]
    return ops, order, end


PLAN = []


def rank_program(g, core, T, topo):
    rank = T.rank_of(core)
    if rank is None:
        return
    if not PLAN:
        PLAN.append(plan())
    ops, order, _end = PLAN[0]
    nr = len(T.cores)
    peer = [T.cores[(rank - 1) % nr], T.cores[(rank + 1) % nr]]

    def masks(src):
        r = T.rank_of(src)
        two = [T.cores[(r - 1) % nr], T.cores[(r + 1) % nr]]
        eng = [topo.engines(src, c) for c in two]
        few = 0 if len(eng[0]) <= len(eng[1]) else 1
        rest = [e for e in eng[1 - few] if e not in eng[few]]
        if not rest:
            half = len(eng[few]) // 2
            rest, eng[few] = eng[few][half:], eng[few][:half]
        eng[1 - few] = rest
        return [sum(1 << e for e in v) for v in eng], [len(v) for v in eng]

    mk, ne = masks(core)
    came = [masks(peer[0])[1][1], masks(peer[1])[1][0]]
    Q = {"V": g.vector, "A": g.scalar, "P": g.tensor, "G": g, "S": g.sync}

    def ap(x):
        if not isinstance(x, dict):
            return x
        v = T[x["n"]][x["i"]]
        return v.indirect(ap(x["off"])) if "off" in x else v

    def token(op):
        if op["k"] == "dma":
            return T.sem["d_" + op["args"][0]], 16
        if op["k"] == "recv":
            k, d, t = op["args"]
            return T.sem["%s%d%d" % (k, d, t)], came[d if k == "m" else 1 - d]
        return T.sem["q" + op["e"]], op["n"]

    total = 0
    for n in order:
        op = ops[n]
        k, args = op["k"], op["args"]
        if k == "recv":
            continue
        q = Q[op["e"]]
        for m in op["w"]:
            q.wait_ge(*token(ops[m]))
        o = ap(op["o"]) if op["o"] is not None else None
        x = [ap(v) for v in op["in"]]
        if k == "dma":
            r = q.dma_start(T[args[0]][:], x[0]) if args[1] else q.dma_start(o, T[args[0]][:])
            r.then_inc(T.sem["d_" + args[0]], 16)
            continue
        if k == "send":
            kind, t = args
            trs = []
            for side in range(2):
                rid, pid, _se = topo.addr(peer[side])
                if kind == "m":
                    d = 1 - side
                    src, dst = T["snd%d" % t][:, d], T["L%d" % t][:, d]
                else:
                    d = side
                    src, dst = T["sm%d" % t][:, 12 + 2 * d:14 + 2 * d], T["ak%d" % t][:, 2 * d:2 * d + 2]
                trs.append(RemoteDMATransfer(dst_ids=[DstId(rid=rid, pnc=pid)], dma_engine_mask=mk[side],
                                             remote_sem=T.sem["%s%d%d" % (kind, d, t)], src=src, dst=dst))
            g.remote_dma_fused(trs, local_sem=T.sem["sent"])
            total += ne[0] + ne[1]
            continue
        if k == "cp":
            r = q.tensor_copy(o, x[0])
        elif k == "ts":
            if args[3] is None:
                r = q.tensor_scalar(o, x[0], ap(args[0]), None, args[1])
            else:
                r = q.tensor_scalar(o, x[0], ap(args[0]), ap(args[2]), args[1], args[3])
        elif k == "tt":
            r = q.tensor_tensor(o, x[0], x[1], args[0])
        elif k == "scan":
            r = q.tensor_tensor_scan(o, x[0], x[1], ap(args[0]), args[1], args[2])
        elif k == "red":
            r = q.tensor_reduce(o, x[0], AxisListType.X, AL.min, apply_absolute_value=True)
        elif k == "ms":
            r = q.memset(o, args[0])
        elif k == "act":
            kw = {}
            if args[1] is not None:
                kw["bias"] = ap(args[1])
            if args[2] is not None:
                kw["scale"] = ap(args[2])
            r = q.activation(o, x[0], args[0], **kw)
        elif k == "mm":
            r = q.matmul(o, x[0], x[1], args[0], args[1])
        elif k == "sel":
            r = q.affine_select(o, x[0], args[0], args[1], args[2], args[3], args[4])
        elif DT[op["o"]["n"]] == i32:
            r = q.iota(o, args[0], args[1], args[2])
        else:
            r = q.iota(o, args[0], args[1], args[2], allow_small_or_imprecise_dtypes=True)
        if op.get("inc"):
            r.then_inc(T.sem["q" + op["e"]], 1)
    g.wait_ge(T.sem["sent"], total)
    g.sync.wait_ge(T.sem["d_yl"], 16)
    g.sync.wait_ge(T.sem["d_yz"], 16)
    g.scalar.wait_ge(T.sem["d_yn"], 16)
